import numpy as np, ml_dtypes
CORES = [37,45,53,61,69,109,117,125]
N = 8
WB, F = 3, 64
def setup_inputs(rng):
    return {"a": rng.standard_normal((N, 128, 128), dtype=np.float32).astype(ml_dtypes.bfloat16), "w": rng.standard_normal((N, 128, F), dtype=np.float32).astype(ml_dtypes.bfloat16)}
def setup_inputs_big(rng):
    d = setup_inputs(rng)
    for k in ("a", "w"): d[k] = (d[k].astype(np.float32) * 1024.0).astype(d[k].dtype)
    return d
def setup_inputs_small(rng):
    d = setup_inputs(rng)
    for k in ("a", "w"): d[k] = (d[k].astype(np.float32) * (1 / 1024.0)).astype(d[k].dtype)
    return d
def setup_inputs_apart(rng):
    d = setup_inputs(rng)
    f = (10.0 ** rng.permutation(np.linspace(-1.5, 1.5, N))).astype(np.float32).reshape(N, 1, 1)
    for k in ("a", "w"): d[k] = (d[k].astype(np.float32) * f).astype(d[k].dtype)
    return d
def reference(a, w):
    A, W = a.astype(np.float64), w.astype(np.float64)
    p = [A[j].T @ W[j] for j in range(N)]
    y = np.stack([sum(p[(r - i) % N] for i in range(WB + 1)) for r in range(N)])
    return {"y": y.astype(ml_dtypes.bfloat16 if a.dtype != np.float64 else np.float64)}

@@ -1,0 +1,123 @@
+from concourse.bass import DstId, RemoteDMATransfer
+from concourse.mybir import AluOpType
+
+WB = 3
+SIM_CORES = 128
+K_ROWS = 4
+K_LONG = 2
+
+SCRATCH = {
+    "a_sb": ("sbuf", [128, 128], "bfloat16"),
+    "w_sb": ("sbuf", [128, 64], "bfloat16"),
+    "acc": ("psum", [128, 64], "float32"),
+    "p_sb": ("sbuf", [128, 64], "bfloat16"),
+    "relay_in": ("dram", [WB, 128, 64], "bfloat16"),
+    "near_in": ("dram", [WB, 128, 64], "bfloat16"),
+    "far_in": ("dram", [128, 64], "bfloat16"),
+}
+SEMAPHORES = ["loaded", "multiplied", "rounded", "sent", "relay", "near", "far", "stored"]
+
+
+def _plan(cores, topo):
+    n = len(cores)
+    plan = []
+    for r in range(n):
+        srcs = [(r - i) % n for i in range(1, WB + 1)]
+        direct = [j for j in srcs if topo.may_write(cores[j], cores[r])]
+        barred = [j for j in srcs if not topo.may_write(cores[j], cores[r])]
+        relay = None
+        if barred:
+            home = cores[barred[0]]
+            taken = [p[2] for p in plan]
+            relay = [c for c in range(SIM_CORES)
+                     if c not in cores and c not in taken
+                     and topo.chip(c) == topo.chip(home) and topo.die(c) == topo.die(home)
+                     and topo.may_write(c, cores[r])
+                     and all(topo.may_write(cores[j], c) for j in barred)][0]
+        plan.append((direct, barred, relay))
+    return plan
+
+
+def _pick(mask, n):
+    bits = [b for b in range(mask.bit_length()) if (mask >> b) & 1]
+    step = len(bits) // n
+    return sum(1 << bits[i * step] for i in range(n))
+
+
+def _dst(topo, c):
+    rid, pid, _ = topo.addr(c)
+    return DstId(rid=rid, pnc=pid)
+
+
+def rank_program(g, core, T, topo):
+    cores = list(T.cores)
+    plan = _plan(cores, topo)
+    sem = T.sem
+    rank = T.rank_of(core)
+
+    for r, (direct, barred, relay) in enumerate(plan):
+        if relay != core:
+            continue
+        g.wait_ge(sem.relay, K_ROWS * len(barred))
+        g.remote_dma_fused(
+            [RemoteDMATransfer(dst_ids=[_dst(topo, cores[r])],
+                               dma_engine_mask=_pick(topo.mask(core, cores[r]), K_LONG),
+                               remote_sem=sem.far,
+                               srcs=[T.relay_in[s] for s in range(len(barred))],
+                               dsts=[T.far_in[:]],
+                               alu_op=1 if len(barred) > 1 else 0)],
+            local_sem=sem.sent)
+        g.wait_ge(sem.sent, K_LONG)
+    if rank is None:
+        return
+
+    g.sync.dma_start(T.a_sb[:], T.a[:]).then_inc(sem.loaded, 16)
+    g.scalar.dma_start(T.w_sb[:], T.w[:]).then_inc(sem.loaded, 16)
+    g.tensor.wait_ge(sem.loaded, 32)
+    g.tensor.matmul(T.acc[:], T.a_sb[:], T.w_sb[:], True, True).then_inc(sem.multiplied, 1)
+    g.vector.wait_ge(sem.multiplied, 1)
+    g.vector.tensor_copy(T.p_sb[:], T.acc[:]).then_inc(sem.rounded, 1)
+    g.wait_ge(sem.rounded, 1)
+
+    to_relay = [(p[2], p[1].index(rank)) for p in plan if rank in p[1]]
+    to_rank = [(cores[r], p[0].index(rank)) for r, p in enumerate(plan) if rank in p[0]]
+    leaving = 0
+    for c, _ in to_relay + to_rank:
+        if topo.chip(c) != topo.chip(core):
+            leaving |= topo.mask(core, c)
+    used = 0
+    sent = 0
+    transfers = []
+    for c, slot in sorted(to_relay, key=lambda cs: topo.chip(cs[0]) == topo.chip(core)):
+        free = topo.mask(core, c) & ~used
+        if topo.chip(c) == topo.chip(core):
+            free &= ~leaving
+        m = _pick(free, K_ROWS)
+        used |= m
+        sent += K_ROWS
+        transfers.append(RemoteDMATransfer(dst_ids=[_dst(topo, c)], dma_engine_mask=m, remote_sem=sem.relay,
+                                           src=T.p_sb[:], dst=T.relay_in[slot]))
+    if transfers:
+        g.remote_dma_fused(transfers, local_sem=sem.sent)
+    for c, slot in to_rank:
+        rid, pid, _ = topo.addr(c)
+        g.remote_dma(out_ap=T.near_in[slot], in_ap=T.p_sb[:], remote_sem=sem.near, local_sem=sem.sent,
+                     pid=pid, routing_id=rid, dma_engine_mask=_pick(topo.mask(core, c), K_ROWS))
+        sent += K_ROWS
+
+    direct, barred, relay = plan[rank]
+    stored = 16
+    g.dma_start(T.y[:], T.p_sb[:]).then_inc(sem.stored, 16)
+    g.wait_ge(sem.stored, stored)
+    if direct:
+        g.wait_ge(sem.near, K_ROWS * len(direct))
+    for s in range(len(direct)):
+        g.dma_start(T.y[:], T.near_in[s], accum_op=AluOpType.add, max_dma_last_dim=4096).then_inc(sem.stored, 16)
+        stored += 16
+        g.wait_ge(sem.stored, stored)
+    if barred:
+        g.wait_ge(sem.far, K_LONG)
+        g.dma_start(T.y[:], T.far_in[:], accum_op=AluOpType.add, max_dma_last_dim=4096).then_inc(sem.stored, 16)
+        stored += 16
+        g.wait_ge(sem.stored, stored)
+    g.wait_ge(sem.sent, sent)

@@ -3,19 +3,20 @@ from concourse.mybir import AluOpType
 
 WB = 3
 SIM_CORES = 128
-K_ROWS = 4
-K_LONG = 2
+K_ROWS = 8
 
 SCRATCH = {
     "a_sb": ("sbuf", [128, 128], "bfloat16"),
     "w_sb": ("sbuf", [128, 64], "bfloat16"),
     "acc": ("psum", [128, 64], "float32"),
+    "acc2": ("psum", [128, 64], "float32"),
     "p_sb": ("sbuf", [128, 64], "bfloat16"),
     "relay_in": ("dram", [WB, 128, 64], "bfloat16"),
-    "near_in": ("dram", [WB, 128, 64], "bfloat16"),
-    "far_in": ("dram", [128, 64], "bfloat16"),
+    "near_in": ("sbuf", [128, 64], "bfloat16"),
+    "far_in": ("sbuf", [128, 64], "bfloat16"),
+    "y_sb": ("sbuf", [128, 64], "bfloat16"),
 }
-SEMAPHORES = ["loaded", "multiplied", "rounded", "sent", "relay", "near", "far", "stored"]
+SEMAPHORES = ["loaded", "multiplied", "rounded", "sent", "relay", "near", "far", "summed", "done", "stored"]
 
 
 def _plan(cores, topo):
@@ -61,13 +62,13 @@ def rank_program(g, core, T, topo):
         g.wait_ge(sem.relay, K_ROWS * len(barred))
         g.remote_dma_fused(
             [RemoteDMATransfer(dst_ids=[_dst(topo, cores[r])],
-                               dma_engine_mask=_pick(topo.mask(core, cores[r]), K_LONG),
+                               dma_engine_mask=_pick(topo.mask(core, cores[r]), K_ROWS),
                                remote_sem=sem.far,
                                srcs=[T.relay_in[s] for s in range(len(barred))],
                                dsts=[T.far_in[:]],
-                               alu_op=1 if len(barred) > 1 else 0)],
+                               alu_op=1)],
             local_sem=sem.sent)
-        g.wait_ge(sem.sent, K_LONG)
+        g.wait_ge(sem.sent, K_ROWS)
     if rank is None:
         return
 
@@ -80,9 +81,9 @@ def rank_program(g, core, T, topo):
     g.wait_ge(sem.rounded, 1)
 
     to_relay = [(p[2], p[1].index(rank)) for p in plan if rank in p[1]]
-    to_rank = [(cores[r], p[0].index(rank)) for r, p in enumerate(plan) if rank in p[0]]
+    to_rank = [cores[r] for r, p in enumerate(plan) if rank in p[0]]
     leaving = 0
-    for c, _ in to_relay + to_rank:
+    for c in [cs[0] for cs in to_relay] + to_rank:
         if topo.chip(c) != topo.chip(core):
             leaving |= topo.mask(core, c)
     used = 0
@@ -97,27 +98,19 @@ def rank_program(g, core, T, topo):
         sent += K_ROWS
         transfers.append(RemoteDMATransfer(dst_ids=[_dst(topo, c)], dma_engine_mask=m, remote_sem=sem.relay,
                                            src=T.p_sb[:], dst=T.relay_in[slot]))
-    if transfers:
-        g.remote_dma_fused(transfers, local_sem=sem.sent)
-    for c, slot in to_rank:
+    g.remote_dma_fused(transfers, local_sem=sem.sent)
+    for c in to_rank:
         rid, pid, _ = topo.addr(c)
-        g.remote_dma(out_ap=T.near_in[slot], in_ap=T.p_sb[:], remote_sem=sem.near, local_sem=sem.sent,
+        g.remote_dma(out_ap=T.near_in[:], in_ap=T.p_sb[:], remote_sem=sem.near, local_sem=sem.sent,
                      pid=pid, routing_id=rid, dma_engine_mask=_pick(topo.mask(core, c), K_ROWS))
         sent += K_ROWS
 
-    direct, barred, relay = plan[rank]
-    stored = 16
-    g.dma_start(T.y[:], T.p_sb[:]).then_inc(sem.stored, 16)
-    g.wait_ge(sem.stored, stored)
-    if direct:
-        g.wait_ge(sem.near, K_ROWS * len(direct))
-    for s in range(len(direct)):
-        g.dma_start(T.y[:], T.near_in[s], accum_op=AluOpType.add, max_dma_last_dim=4096).then_inc(sem.stored, 16)
-        stored += 16
-        g.wait_ge(sem.stored, stored)
-    if barred:
-        g.wait_ge(sem.far, K_LONG)
-        g.dma_start(T.y[:], T.far_in[:], accum_op=AluOpType.add, max_dma_last_dim=4096).then_inc(sem.stored, 16)
-        stored += 16
-        g.wait_ge(sem.stored, stored)
+    g.vector.wait_ge(sem.near, K_ROWS)
+    g.vector.tensor_tensor(T.acc2[:], T.acc[:], T.near_in[:], AluOpType.add).then_inc(sem.summed, 1)
+    g.vector.wait_ge(sem.summed, 1)
+    g.vector.wait_ge(sem.far, K_ROWS)
+    g.vector.tensor_tensor(T.y_sb[:], T.acc2[:], T.far_in[:], AluOpType.add).then_inc(sem.done, 1)
+    g.sync.wait_ge(sem.done, 1)
+    g.sync.dma_start(T.y[:], T.y_sb[:]).then_inc(sem.stored, 16)
+    g.sync.wait_ge(sem.stored, 16)
     g.wait_ge(sem.sent, sent)

from concourse.bass import DstId, RemoteDMATransfer
from concourse.mybir import AluOpType

WB = 3
SIM_CORES = 128
K_ROWS = 8

SCRATCH = {
    "a_sb": ("sbuf", [128, 128], "bfloat16"),
    "w_sb": ("sbuf", [128, 64], "bfloat16"),
    "acc": ("psum", [128, 64], "float32"),
    "acc2": ("psum", [128, 64], "float32"),
    "p_sb": ("sbuf", [128, 64], "bfloat16"),
    "relay_in": ("dram", [WB, 128, 64], "bfloat16"),
    "near_in": ("sbuf", [128, 64], "bfloat16"),
    "far_in": ("sbuf", [128, 64], "bfloat16"),
    "y_sb": ("sbuf", [128, 64], "bfloat16"),
}
SEMAPHORES = ["loaded", "multiplied", "rounded", "sent", "relay", "near", "far", "summed", "done", "stored"]


def _plan(cores, topo):
    n = len(cores)
    plan = []
    for r in range(n):
        srcs = [(r - i) % n for i in range(1, WB + 1)]
        direct = [j for j in srcs if topo.may_write(cores[j], cores[r])]
        barred = [j for j in srcs if not topo.may_write(cores[j], cores[r])]
        relay = None
        if barred:
            home = cores[barred[0]]
            taken = [p[2] for p in plan]
            relay = [c for c in range(SIM_CORES)
                     if c not in cores and c not in taken
                     and topo.chip(c) == topo.chip(home) and topo.die(c) == topo.die(home)
                     and topo.may_write(c, cores[r])
                     and all(topo.may_write(cores[j], c) for j in barred)][0]
        plan.append((direct, barred, relay))
    return plan


def _pick(mask, n):
    bits = [b for b in range(mask.bit_length()) if (mask >> b) & 1]
    step = len(bits) // n
    return sum(1 << bits[i * step] for i in range(n))


def _dst(topo, c):
    rid, pid, _ = topo.addr(c)
    return DstId(rid=rid, pnc=pid)


def rank_program(g, core, T, topo):
    cores = list(T.cores)
    plan = _plan(cores, topo)
    sem = T.sem
    rank = T.rank_of(core)

    for r, (direct, barred, relay) in enumerate(plan):
        if relay != core:
            continue
        g.wait_ge(sem.relay, K_ROWS * len(barred))
        g.remote_dma_fused(
            [RemoteDMATransfer(dst_ids=[_dst(topo, cores[r])],
                               dma_engine_mask=_pick(topo.mask(core, cores[r]), K_ROWS),
                               remote_sem=sem.far,
                               srcs=[T.relay_in[s] for s in range(len(barred))],
                               dsts=[T.far_in[:]],
                               alu_op=1)],
            local_sem=sem.sent)
        g.wait_ge(sem.sent, K_ROWS)
    if rank is None:
        return

    g.sync.dma_start(T.a_sb[:], T.a[:]).then_inc(sem.loaded, 16)
    g.scalar.dma_start(T.w_sb[:], T.w[:]).then_inc(sem.loaded, 16)
    g.tensor.wait_ge(sem.loaded, 32)
    g.tensor.matmul(T.acc[:], T.a_sb[:], T.w_sb[:], True, True).then_inc(sem.multiplied, 1)
    g.vector.wait_ge(sem.multiplied, 1)
    g.vector.tensor_copy(T.p_sb[:], T.acc[:]).then_inc(sem.rounded, 1)
    g.wait_ge(sem.rounded, 1)

    to_relay = [(p[2], p[1].index(rank)) for p in plan if rank in p[1]]
    to_rank = [cores[r] for r, p in enumerate(plan) if rank in p[0]]
    leaving = 0
    for c in [cs[0] for cs in to_relay] + to_rank:
        if topo.chip(c) != topo.chip(core):
            leaving |= topo.mask(core, c)
    used = 0
    sent = 0
    transfers = []
    for c, slot in sorted(to_relay, key=lambda cs: topo.chip(cs[0]) == topo.chip(core)):
        free = topo.mask(core, c) & ~used
        if topo.chip(c) == topo.chip(core):
            free &= ~leaving
        m = _pick(free, K_ROWS)
        used |= m
        sent += K_ROWS
        transfers.append(RemoteDMATransfer(dst_ids=[_dst(topo, c)], dma_engine_mask=m, remote_sem=sem.relay,
                                           src=T.p_sb[:], dst=T.relay_in[slot]))
    g.remote_dma_fused(transfers, local_sem=sem.sent)
    for c in to_rank:
        rid, pid, _ = topo.addr(c)
        g.remote_dma(out_ap=T.near_in[:], in_ap=T.p_sb[:], remote_sem=sem.near, local_sem=sem.sent,
                     pid=pid, routing_id=rid, dma_engine_mask=_pick(topo.mask(core, c), K_ROWS))
        sent += K_ROWS

    g.vector.wait_ge(sem.near, K_ROWS)
    g.vector.tensor_tensor(T.acc2[:], T.acc[:], T.near_in[:], AluOpType.add).then_inc(sem.summed, 1)
    g.vector.wait_ge(sem.summed, 1)
    g.vector.wait_ge(sem.far, K_ROWS)
    g.vector.tensor_tensor(T.y_sb[:], T.acc2[:], T.far_in[:], AluOpType.add).then_inc(sem.done, 1)
    g.sync.wait_ge(sem.done, 1)
    g.sync.dma_start(T.y[:], T.y_sb[:]).then_inc(sem.stored, 16)
    g.sync.wait_ge(sem.stored, 16)
    g.wait_ge(sem.sent, sent)
